import numpy as np
import ml_dtypes


def mxq(x, axis, fmt="e4m3"):
    dtype, down = {"e4m3": (ml_dtypes.float8_e4m3fn, 7), "e5m2": (ml_dtypes.float8_e5m2, 14)}[fmt]
    v = np.moveaxis(np.asarray(x, np.float32).astype(ml_dtypes.bfloat16).astype(np.float64), axis, -1)
    blocks = v.reshape(v.shape[:-1] + (-1, 32))
    amax = np.abs(blocks).max(-1, keepdims=True)
    byte = np.maximum(np.where(amax > 0, np.frexp(amax)[1] - 1 + 127, 0) - down, 1)
    scale = np.exp2(byte - 127.0)
    codes = (blocks / scale).astype(np.float32).astype(dtype).astype(np.float64)
    return np.moveaxis((codes * scale).reshape(v.shape), -1, axis)


WIDE = False


def mx_kscale(k):
    if not WIDE:
        return np.ones(k)
    levels = np.array([10, -10, 5, -5, 0])
    if k % 512:
        return np.exp2(np.random.permutation(np.resize(levels, k // 32))).repeat(32)
    a = np.empty((k // 512, 16))
    for p in range(k // 512):
        a[p, :8] = np.random.permutation(np.resize(levels, 8))
        for g in range(8):
            far = levels[np.abs(levels - a[p, g]) >= 10]
            a[p, g + 8] = far[np.random.randint(len(far))]
    return np.exp2(a.ravel()).repeat(32)


def f64(x):
    return np.asarray(x).astype(np.float64)


def striped(idx):
    return np.tile(np.asarray(idx).reshape(-1, 16).T, (8, 1)).astype(np.uint16)


def unstriped(offs):
    return offs[:16].T.reshape(-1).astype(np.int64)


E2M1 = np.array([0.0, 0.5, 1.0, 1.5, 2.0, 3.0, 4.0, 6.0, -0.0, -0.5, -1.0, -1.5, -2.0, -3.0, -4.0, -6.0])


def pack_weight(w, fmt):
    k, n = w.shape
    w = f64(np.asarray(w, np.float32).astype(ml_dtypes.bfloat16)).reshape(k // 32, 32, n)
    amax = np.abs(w).max(1)
    if fmt == "e4m3":
        byte = np.frexp(amax)[1] - 1 + 127 - 7
    else:
        mant, ex = np.frexp(amax / 6.0)
        byte = np.where(mant > 0.5, ex, ex - 1) + 127
    byte = np.clip(np.where(amax > 0, byte, 1), 1, 254)
    scaled = (w * np.exp2(127.0 - byte)[:, None, :]).reshape(k, n).astype(np.float32)
    by_word = np.ascontiguousarray(scaled.reshape(k // 512, 128, 4, n).transpose(0, 1, 3, 2))
    if fmt == "e4m3":
        words = by_word.astype(ml_dtypes.float8_e4m3fn).view(np.uint8)
    else:
        c = by_word.astype(ml_dtypes.float4_e2m1fn).view(np.uint8) & 0xF
        words = (c[..., 0::2] | (c[..., 1::2] << 4)).reshape(k // 512, 128, 2 * n)
    return np.ascontiguousarray(words), np.ascontiguousarray(byte.astype(np.uint8).reshape(k // 512, 16, n))


def unpack_weight(words, scales, fmt):
    g, _, n = scales.shape
    words = np.ascontiguousarray(words).reshape(g, 128, n, -1)
    if fmt == "e4m3":
        vals = words.view(ml_dtypes.float8_e4m3fn).astype(np.float64)
    else:
        nib = np.empty((g, 128, n, 4), np.uint8)
        nib[..., 0::2] = words & 0xF
        nib[..., 1::2] = words >> 4
        vals = E2M1[nib]
    vals = vals * np.repeat(np.exp2(scales.astype(np.float64) - 127.0), 8, axis=1)[..., None]
    return vals.transpose(0, 1, 3, 2).reshape(g * 512, n)


def sigmoid(v):
    return 1.0 / (1.0 + np.exp(-v))


def sgn(shape):
    return np.random.uniform(0.5, 2.0, shape) * np.where(np.random.standard_normal(shape) < 0, -1.0, 1.0)


K, T, J, R, F, Z, O, Q, N, E = 512, 1024, 256, 512, 512, 1024, 128, 128, 256, 256


def setup_inputs():
    n = np.random.standard_normal
    idx = np.random.permutation(T)[:J]
    idx2 = np.random.permutation(Z)[:J]
    idx3 = np.random.permutation(J)[:O]
    idx4 = np.random.permutation(J)[:O]
    idx5 = np.random.permutation(J)[:O]
    idx6 = np.random.permutation(J)[:O]
    idx7 = np.random.permutation(E)[:O]
    fk = mx_kscale(K)
    ff = mx_kscale(F)
    fr = mx_kscale(R)
    fr = fr / fr.max()
    xtp = pack_weight(n((K, T)) / fk[:, None], "e4m3")
    xop = pack_weight(n((F, Z)) / ff[:, None], "e2m1")
    wp = pack_weight(n((K, R)) * 1 / np.sqrt(K) * fk[:, None], "e2m1")
    w0p = pack_weight(n((F, R)) * 1 / np.sqrt(F) * ff[:, None], "e4m3")
    wbp = pack_weight(n((R, N)) * 1 / np.sqrt(R) / fr[:, None], "e4m3")
    return {
        "xt_words": xtp[0],
        "xt_scales": xtp[1],
        "xo_words": xop[0],
        "xo_scales": xop[1],
        "w_words": wp[0],
        "w_scales": wp[1],
        "w0_words": w0p[0],
        "w0_scales": w0p[1],
        "sa": (np.random.uniform(0.5, 1.6, (Q, 1)) * fr[::4, None]).astype(np.float32),
        "sb": (sgn((Q, 1)) * fr[::4, None]).astype(np.float32),
        "sd": (0.2 * sgn((Q, 1))).astype(np.float32),
        "bd": (np.random.uniform(-0.5, 0.3, (Q, 1)) + np.log(fr[::4])[:, None]).astype(np.float32),
        "se": (0.4 * sgn((Q, 1))).astype(np.float32),
        "be": (np.random.uniform(-2.2, 0.2, (Q, 1)) + np.log(fr[::4])[:, None]).astype(np.float32),
        "wb_words": wbp[0],
        "wb_scales": wbp[1],
        "so": (np.random.uniform(0.5, 1.6, (N, 1))).astype(np.float32),
        "offs": striped(idx),
        "offs2": striped(idx2),
        "offs3": striped(idx3),
        "offs4": striped(idx4),
        "offs5": striped(idx5),
        "offs6": striped(idx6),
        "offs7": striped(idx7),
    }


def reference(xt_words, xt_scales, xo_words, xo_scales, w_words, w_scales, w0_words, w0_scales, sa, sb, sd, bd, se, be, wb_words, wb_scales, so, offs, offs2, offs3, offs4, offs5, offs6, offs7):
    idx = unstriped(offs)
    idx2 = unstriped(offs2)
    idx3 = unstriped(offs3)
    idx4 = unstriped(offs4)
    idx5 = unstriped(offs5)
    idx6 = unstriped(offs6)
    idx7 = unstriped(offs7)
    xtu = unpack_weight(xt_words, xt_scales, "e4m3")
    xou = unpack_weight(xo_words, xo_scales, "e2m1")
    wu = unpack_weight(w_words, w_scales, "e2m1")
    w0u = unpack_weight(w0_words, w0_scales, "e4m3")
    wbu = unpack_weight(wb_words, wb_scales, "e4m3")
    xtidxg = xtu[:, idx]
    xoidx2g = xou[:, idx2]
    a = wu.T @ xtidxg + w0u.T @ xoidx2g
    a0 = a[0::4]
    a1 = a[1::4]
    a2 = a[2::4]
    a3 = a[3::4]
    v0 = a0[:, idx3] * f64(sa)
    v1 = a1[:, idx4] * f64(sb)
    v2 = np.exp(a2[:, idx5] * f64(sd) + f64(bd))
    v3 = sigmoid(a3[:, idx6] * f64(se) + f64(be))
    hid = np.stack([v0, v1, v2, v3], axis=1).reshape(R, O)
    hidq = mxq(hid, 0, "e4m3")
    p = wbu.T @ hidq
    y = np.zeros((N, E))
    y[:, idx7] = p * f64(so)
    return y

@@ -1,0 +1,151 @@
+from contextlib import ExitStack
+
+import concourse.mybir as mybir
+
+F32 = mybir.dt.float32
+BF16 = mybir.dt.bfloat16
+I32 = mybir.dt.int32
+U32 = mybir.dt.uint32
+U16 = mybir.dt.uint16
+U8 = mybir.dt.uint8
+E4M3X4 = mybir.dt.float8_e4m3fn_x4
+E2M1X4 = mybir.dt.float4_e2m1fn_x4
+ACT = mybir.ActivationFunctionType
+
+P = 128
+T, J, R, O, N, E = 1024, 256, 512, 128, 256, 256
+QUARTERS = 4
+QUADRANTS = 4
+FLOPS = 2 * 512 * R * J * 2 + 2 * R * N * O
+
+
+def load_scale_rows(queues, plane, scales):
+    for quad in range(QUADRANTS):
+        queues[quad].dma_start(
+            out=plane[32 * quad : 32 * quad + 4, :].bitcast(I32),
+            in_=scales[0, 4 * quad : 4 * quad + 4, :].bitcast(I32),
+        )
+
+
+def tile_list_quarterlaws_kernel(
+    tc, xt_words, xt_scales, xo_words, xo_scales, w_words, w_scales, w0_words, w0_scales,
+    sa, sb, sd, bd, se, be, wb_words, wb_scales, so,
+    offs, offs2, offs3, offs4, offs5, offs6, offs7, out,
+):
+    nc = tc.nc
+    with ExitStack() as ctx:
+        sb_pool = ctx.enter_context(tc.tile_pool(name="held", bufs=1))
+        psum = ctx.enter_context(tc.psum_pool(name="psum", bufs=1))
+
+        def held(name, shape, dtype):
+            return sb_pool.tile(shape, dtype, name=name, align_bytes=64)
+
+        def load_list(name, src):
+            lst = held(name, list(src.shape), U16)
+            nc.sync.dma_start(lst[:], src)
+            return lst
+
+        def load_column(queue, name, src):
+            col = held(name, [P, 1], F32)
+            queue.dma_start(out=col[:], in_=src)
+            return col
+
+        xt_w = held("xt_w", [P, T], U32)
+        xo_w = held("xo_w", [P, T], U16)
+        w_w = held("w_w", [P, R], U16)
+        w0_w = held("w0_w", [P, R], U32)
+        wb_w = held("wb_w", [P, N], U32)
+        xt_s = held("xt_s", [P, T], U8)
+        xo_s = held("xo_s", [P, T], U8)
+        w_s = held("w_s", [P, R], U8)
+        w0_s = held("w0_s", [P, R], U8)
+        wb_s = held("wb_s", [P, N], U8)
+        pages = [held("page%d" % t, [P, E], F32) for t in range(N // P)]
+
+        for plane in (xt_s, w_s, xo_s, w0_s, wb_s):
+            nc.vector.memset(plane[:].bitcast(I32), 0)
+        for page in pages:
+            nc.vector.memset(page[:], 0.0)
+
+        sy, sc, gp = nc.sync, nc.scalar, nc.gpsimd
+        load_scale_rows([gp] * 4, w_s, w_scales)
+        idx = load_list("idx", offs)
+        sc.dma_start(out=xt_w[:].bitcast(I32), in_=xt_words[0].rearrange("p c r -> p (c r)").bitcast(I32))
+        load_scale_rows([sy, sc, sy, sc], xt_s, xt_scales)
+        idx2 = load_list("idx2", offs2)
+        sc.dma_start(out=xo_w[:].bitcast(I32), in_=xo_words[0].bitcast(I32))
+        load_scale_rows([sy] * 4, xo_s, xo_scales)
+        sc.dma_start(out=w0_w[:].bitcast(I32), in_=w0_words[0].rearrange("p c r -> p (c r)").bitcast(I32))
+        sc.dma_start(out=w_w[:].bitcast(I32), in_=w_words[0].bitcast(I32))
+        load_scale_rows([sc, sc, sy, sy], w0_s, w0_scales)
+        idx5 = load_list("idx5", offs5)
+        sd_c = load_column(nc.sync, "sd_c", sd)
+        bd_c = load_column(nc.sync, "bd_c", bd)
+        idx6 = load_list("idx6", offs6)
+        se_c = load_column(nc.sync, "se_c", se)
+        be_c = load_column(nc.sync, "be_c", be)
+        idx3 = load_list("idx3", offs3)
+        idx4 = load_list("idx4", offs4)
+        nc.sync.dma_start(out=wb_w[:].bitcast(I32), in_=wb_words[0].rearrange("p c r -> p (c r)").bitcast(I32))
+        idx7 = load_list("idx7", offs7)
+        sa_c = load_column(nc.gpsimd, "sa_c", sa)
+        sb_c = load_column(nc.gpsimd, "sb_c", sb)
+        load_scale_rows([gp] * 4, wb_s, wb_scales)
+        so_c = held("so_c", [P, N // P, 1], F32)
+        nc.gpsimd.dma_start(out=so_c[:], in_=so.rearrange("(t p) o -> p t o", p=P))
+
+        xt_sg = held("xt_sg", [P, J], U8)
+        xt_wg = held("xt_wg", [P, J], U32)
+        xo_sg = held("xo_sg", [P, J], U8)
+        xo_wg = held("xo_wg", [P, J], U16)
+        nc.vector.tensor_copy(xt_sg[:], xt_s[:].indirect(idx[:]))
+        nc.vector.tensor_copy(xt_wg[:], xt_w[:].indirect(idx[:]))
+        nc.vector.tensor_copy(xo_wg[:], xo_w[:].indirect(idx2[:]))
+        nc.vector.tensor_copy(xo_sg[:], xo_s[:].indirect(idx2[:]))
+
+        def deal(copy, name, src, dtype):
+            dealt = held(name, [P, QUARTERS, P], dtype)
+            copy(out=dealt[:].rearrange("p g q -> p q g"), in_=src[:].rearrange("p (q g) -> p q g", g=QUARTERS))
+            return dealt
+
+        w0_wd = deal(nc.scalar.copy, "w0_wd", w0_w, U32)
+        w_wd = deal(nc.scalar.copy, "w_wd", w_w, U16)
+        w_sd = deal(nc.vector.tensor_copy, "w_sd", w_s, U8)
+        w0_sd = deal(nc.vector.tensor_copy, "w0_sd", w0_s, U8)
+
+        hid = held("hid", [P, O * QUARTERS], BF16)
+        laws = (
+            (2, idx5, ACT.Exp, dict(scale=sd_c[:], bias=bd_c[:])),
+            (3, idx6, ACT.Sigmoid, dict(scale=se_c[:], bias=be_c[:])),
+            (0, idx3, ACT.Copy, dict(scale=sa_c[:])),
+            (1, idx4, ACT.Copy, dict(scale=sb_c[:])),
+        )
+        for g, lst, func, affine in laws:
+            acc = psum.tile([P, J], F32, name="acc%d" % g)
+            nc.tensor.matmul_mx(
+                out=acc[:], lhsT=w0_wd[:, g, :].bitcast(E4M3X4), lhsT_scale=w0_sd[:, g, :],
+                rhs=xo_wg[:].bitcast(E2M1X4), rhs_scale=xo_sg[:], start=True, stop=False,
+            )
+            nc.tensor.matmul_mx(
+                out=acc[:], lhsT=w_wd[:, g, :].bitcast(E2M1X4), lhsT_scale=w_sd[:, g, :],
+                rhs=xt_wg[:].bitcast(E4M3X4), rhs_scale=xt_sg[:], start=False, stop=True,
+            )
+            a_g = held("a%d" % g, [P, J], F32)
+            nc.vector.tensor_copy(a_g[:], acc[:])
+            nc.scalar.activation(out=hid[:, g : O * QUARTERS : QUARTERS], in_=a_g[:].indirect(lst[:]), func=func, **affine)
+
+        hid_w = held("hid_w", [P, O], U32)
+        hid_s = held("hid_s", [P, O], U8)
+        nc.vector.quantize_mx(out=hid_w[:].bitcast(E4M3X4), scales=hid_s[:], in_=hid[:])
+
+        for t in range(N // P):
+            cols = slice(t * P, (t + 1) * P)
+            acc = psum.tile([P, O], F32, name="pacc%d" % t)
+            nc.tensor.matmul_mx(
+                out=acc[:], lhsT=wb_w[:, cols].bitcast(E4M3X4), lhsT_scale=wb_s[:, cols],
+                rhs=hid_w[:].bitcast(E4M3X4), rhs_scale=hid_s[:], start=True, stop=True,
+            )
+            p_t = held("p%d" % t, [P, O], F32)
+            nc.vector.tensor_copy(p_t[:], acc[:])
+            nc.scalar.activation(out=pages[t][:].indirect(idx7[:]), in_=p_t[:], func=ACT.Copy, scale=so_c[:, t, :])
+            nc.sync.dma_start(out=out[cols, :], in_=pages[t][:])

@@ -16,15 +16,33 @@ P = 128
 T, J, R, O, N, E = 1024, 256, 512, 128, 256, 256
 QUARTERS = 4
 QUADRANTS = 4
+HALF = O // 2
 FLOPS = 2 * 512 * R * J * 2 + 2 * R * N * O
 
 
-def load_scale_rows(queues, plane, scales):
-    for quad in range(QUADRANTS):
-        queues[quad].dma_start(
+def load_scale_rows(queue, plane, scales, quadrants):
+    for quad in quadrants:
+        queue.dma_start(
+            out=plane[32 * quad : 32 * quad + 32, :].bitcast(I32),
+            in_=scales[:, 4 * quad : 4 * quad + 4, :].bitcast(I32).to_broadcast([8, 4, scales.shape[2] // 4]),
+        )
+
+
+def load_live_scale_rows(queue, plane, scales, quadrants):
+    for quad in quadrants:
+        queue.dma_start(
             out=plane[32 * quad : 32 * quad + 4, :].bitcast(I32),
             in_=scales[0, 4 * quad : 4 * quad + 4, :].bitcast(I32),
         )
+
+
+def stage_scale_rows(queue, stage, scales):
+    queue.dma_start(out=stage, in_=scales[0].bitcast(I32).rearrange("(a r) c -> r a c", r=4))
+
+
+def spread_scale_rows(nc, plane, stage):
+    for quad in range(QUADRANTS):
+        nc.vector.tensor_copy(plane[32 * quad : 32 * quad + 4, :].bitcast(I32), stage[:, quad, :])
 
 
 def tile_list_quarterlaws_kernel(
@@ -57,61 +75,68 @@ def tile_list_quarterlaws_kernel(
         wb_w = held("wb_w", [P, N], U32)
         xt_s = held("xt_s", [P, T], U8)
         xo_s = held("xo_s", [P, T], U8)
-        w_s = held("w_s", [P, R], U8)
-        w0_s = held("w0_s", [P, R], U8)
+        ww_s = held("ww_s", [P, 2 * R], U8)
+        ww_stage = held("ww_stage", [4, QUADRANTS, 2 * R // 4], I32)
+        wb_stage = held("wb_stage", [4, QUADRANTS, N // 4], I32)
         wb_s = held("wb_s", [P, N], U8)
         pages = [held("page%d" % t, [P, E], F32) for t in range(N // P)]
 
-        for plane in (xt_s, w_s, xo_s, w0_s, wb_s):
+        nc.vector.memset(xo_s[0:64, :].bitcast(I32), 0)
+        nc.vector.memset(xo_s[64:96, :].bitcast(I32), 0)
+        for plane in (ww_s, wb_s):
             nc.vector.memset(plane[:].bitcast(I32), 0)
         for page in pages:
             nc.vector.memset(page[:], 0.0)
 
-        sy, sc, gp = nc.sync, nc.scalar, nc.gpsimd
-        load_scale_rows([gp] * 4, w_s, w_scales)
+        sy, gp = nc.sync, nc.gpsimd
+        stage_scale_rows(sy, ww_stage[:, :, 0 : R // 4], w_scales)
+        stage_scale_rows(sy, ww_stage[:, :, R // 4 : 2 * R // 4], w0_scales)
         idx = load_list("idx", offs)
-        sc.dma_start(out=xt_w[:].bitcast(I32), in_=xt_words[0].rearrange("p c r -> p (c r)").bitcast(I32))
-        load_scale_rows([sy, sc, sy, sc], xt_s, xt_scales)
+        load_scale_rows(sy, xt_s, xt_scales, (0, 1, 2, 3))
+        sy.dma_start(out=xt_w[:].bitcast(I32), in_=xt_words[0].rearrange("p c r -> p (c r)").bitcast(I32))
         idx2 = load_list("idx2", offs2)
-        sc.dma_start(out=xo_w[:].bitcast(I32), in_=xo_words[0].bitcast(I32))
-        load_scale_rows([sy] * 4, xo_s, xo_scales)
-        sc.dma_start(out=w0_w[:].bitcast(I32), in_=w0_words[0].rearrange("p c r -> p (c r)").bitcast(I32))
-        sc.dma_start(out=w_w[:].bitcast(I32), in_=w_words[0].bitcast(I32))
-        load_scale_rows([sc, sc, sy, sy], w0_s, w0_scales)
+        sy.dma_start(out=xo_w[:].bitcast(I32), in_=xo_words[0].bitcast(I32))
+        sy.dma_start(out=w_w[:].bitcast(I32), in_=w_words[0].bitcast(I32))
+        load_live_scale_rows(sy, xo_s, xo_scales, (0, 1, 2))
+        load_scale_rows(gp, xo_s, xo_scales, (3,))
+        sy.dma_start(out=w0_w[:].bitcast(I32), in_=w0_words[0].rearrange("p c r -> p (c r)").bitcast(I32))
         idx5 = load_list("idx5", offs5)
-        sd_c = load_column(nc.sync, "sd_c", sd)
-        bd_c = load_column(nc.sync, "bd_c", bd)
+        sd_c = load_column(sy, "sd_c", sd)
+        bd_c = load_column(sy, "bd_c", bd)
         idx6 = load_list("idx6", offs6)
-        se_c = load_column(nc.sync, "se_c", se)
-        be_c = load_column(nc.sync, "be_c", be)
+        se_c = load_column(sy, "se_c", se)
+        be_c = load_column(sy, "be_c", be)
         idx3 = load_list("idx3", offs3)
         idx4 = load_list("idx4", offs4)
-        nc.sync.dma_start(out=wb_w[:].bitcast(I32), in_=wb_words[0].rearrange("p c r -> p (c r)").bitcast(I32))
+        stage_scale_rows(sy, wb_stage[:], wb_scales)
+        sy.dma_start(out=wb_w[:].bitcast(I32), in_=wb_words[0].rearrange("p c r -> p (c r)").bitcast(I32))
         idx7 = load_list("idx7", offs7)
-        sa_c = load_column(nc.gpsimd, "sa_c", sa)
-        sb_c = load_column(nc.gpsimd, "sb_c", sb)
-        load_scale_rows([gp] * 4, wb_s, wb_scales)
+        sa_c = load_column(gp, "sa_c", sa)
+        sb_c = load_column(gp, "sb_c", sb)
         so_c = held("so_c", [P, N // P, 1], F32)
-        nc.gpsimd.dma_start(out=so_c[:], in_=so.rearrange("(t p) o -> p t o", p=P))
+        gp.dma_start(out=so_c[:], in_=so.rearrange("(t p) o -> p t o", p=P))
 
+        spread_scale_rows(nc, ww_s, ww_stage)
         xt_sg = held("xt_sg", [P, J], U8)
         xt_wg = held("xt_wg", [P, J], U32)
         xo_sg = held("xo_sg", [P, J], U8)
         xo_wg = held("xo_wg", [P, J], U16)
         nc.vector.tensor_copy(xt_sg[:], xt_s[:].indirect(idx[:]))
+        ww_sd = held("ww_sd", [P, 2, QUARTERS, P], U8)
+        nc.vector.tensor_copy(
+            out=ww_sd[:].rearrange("p m g q -> p m q g"),
+            in_=ww_s[:].rearrange("p (m q g) -> p m q g", m=2, g=QUARTERS),
+        )
         nc.vector.tensor_copy(xt_wg[:], xt_w[:].indirect(idx[:]))
         nc.vector.tensor_copy(xo_wg[:], xo_w[:].indirect(idx2[:]))
         nc.vector.tensor_copy(xo_sg[:], xo_s[:].indirect(idx2[:]))
 
-        def deal(copy, name, src, dtype):
-            dealt = held(name, [P, QUARTERS, P], dtype)
-            copy(out=dealt[:].rearrange("p g q -> p q g"), in_=src[:].rearrange("p (q g) -> p q g", g=QUARTERS))
-            return dealt
-
-        w0_wd = deal(nc.scalar.copy, "w0_wd", w0_w, U32)
-        w_wd = deal(nc.scalar.copy, "w_wd", w_w, U16)
-        w_sd = deal(nc.vector.tensor_copy, "w_sd", w_s, U8)
-        w0_sd = deal(nc.vector.tensor_copy, "w0_sd", w0_s, U8)
+        w_wd = held("w_wd", [P, QUARTERS, P], U16)
+        nc.scalar.copy(out=w_wd[:].rearrange("p g q -> p q g"), in_=w_w[:].rearrange("p (q g) -> p q g", g=QUARTERS))
+        w0_wd = {}
+        for g in (2, 3, 0, 1):
+            w0_wd[g] = held("w0_wd%d" % g, [P, P], U32)
+            nc.scalar.copy(out=w0_wd[g][:], in_=w0_w[:, g:R:QUARTERS])
 
         hid = held("hid", [P, O * QUARTERS], BF16)
         laws = (
@@ -120,32 +145,54 @@ def tile_list_quarterlaws_kernel(
             (0, idx3, ACT.Copy, dict(scale=sa_c[:])),
             (1, idx4, ACT.Copy, dict(scale=sb_c[:])),
         )
+        acc_of = {}
         for g, lst, func, affine in laws:
-            acc = psum.tile([P, J], F32, name="acc%d" % g)
+            acc_of[g] = psum.tile([P, J], F32, name="acc%d" % g)
             nc.tensor.matmul_mx(
-                out=acc[:], lhsT=w0_wd[:, g, :].bitcast(E4M3X4), lhsT_scale=w0_sd[:, g, :],
-                rhs=xo_wg[:].bitcast(E2M1X4), rhs_scale=xo_sg[:], start=True, stop=False,
+                out=acc_of[g][:], lhsT=w_wd[:, g, :].bitcast(E2M1X4), lhsT_scale=ww_sd[:, 0, g, :],
+                rhs=xt_wg[:].bitcast(E4M3X4), rhs_scale=xt_sg[:], start=True, stop=False,
             )
+        a_of = {}
+        for g, lst, func, affine in laws:
             nc.tensor.matmul_mx(
-                out=acc[:], lhsT=w_wd[:, g, :].bitcast(E2M1X4), lhsT_scale=w_sd[:, g, :],
-                rhs=xt_wg[:].bitcast(E4M3X4), rhs_scale=xt_sg[:], start=False, stop=True,
+                out=acc_of[g][:], lhsT=w0_wd[g][:].bitcast(E4M3X4), lhsT_scale=ww_sd[:, 1, g, :],
+                rhs=xo_wg[:].bitcast(E2M1X4), rhs_scale=xo_sg[:], start=False, stop=True,
             )
-            a_g = held("a%d" % g, [P, J], F32)
-            nc.vector.tensor_copy(a_g[:], acc[:])
-            nc.scalar.activation(out=hid[:, g : O * QUARTERS : QUARTERS], in_=a_g[:].indirect(lst[:]), func=func, **affine)
+            a_of[g] = held("a%d" % g, [P, J], F32)
+            nc.vector.tensor_copy(a_of[g][:], acc_of[g][:])
 
-        hid_w = held("hid_w", [P, O], U32)
-        hid_s = held("hid_s", [P, O], U8)
-        nc.vector.quantize_mx(out=hid_w[:].bitcast(E4M3X4), scales=hid_s[:], in_=hid[:])
+        def fetch(law, first, count):
+            g, lst, func, affine = law
+            nc.scalar.activation(
+                out=hid[:, QUARTERS * first + g : QUARTERS * (first + count) : QUARTERS],
+                in_=a_of[g][:].indirect(lst[:, first // 16 : (first + count) // 16]), func=func, **affine,
+            )
 
+        fetch(laws[0], 0, O)
+        for half in range(2):
+            for law in laws[1:]:
+                fetch(law, half * HALF, HALF)
+
+        spread_scale_rows(nc, wb_s, wb_stage)
+        for half in range(2):
+            hid_w = held("hid_w%d" % half, [P, HALF], U32)
+            hid_s = held("hid_s%d" % half, [P, HALF], U8)
+            nc.vector.quantize_mx(
+                out=hid_w[:].bitcast(E4M3X4), scales=hid_s[:],
+                in_=hid[:, QUARTERS * HALF * half : QUARTERS * HALF * (half + 1)],
+            )
+            for t in range(N // P):
+                cols = slice(t * P, (t + 1) * P)
+                acc = psum.tile([P, HALF], F32, name="pacc%d%d" % (half, t))
+                nc.tensor.matmul_mx(
+                    out=acc[:], lhsT=wb_w[:, cols].bitcast(E4M3X4), lhsT_scale=wb_s[:, cols],
+                    rhs=hid_w[:].bitcast(E4M3X4), rhs_scale=hid_s[:], start=True, stop=True,
+                )
+                p_part = held("p%d%d" % (half, t), [P, HALF], F32)
+                nc.vector.tensor_copy(p_part[:], acc[:])
+                nc.scalar.activation(
+                    out=pages[t][:].indirect(idx7[:, half * HALF // 16 : (half + 1) * HALF // 16]),
+                    in_=p_part[:], func=ACT.Copy, scale=so_c[:, t, :],
+                )
         for t in range(N // P):
-            cols = slice(t * P, (t + 1) * P)
-            acc = psum.tile([P, O], F32, name="pacc%d" % t)
-            nc.tensor.matmul_mx(
-                out=acc[:], lhsT=wb_w[:, cols].bitcast(E4M3X4), lhsT_scale=wb_s[:, cols],
-                rhs=hid_w[:].bitcast(E4M3X4), rhs_scale=hid_s[:], start=True, stop=True,
-            )
-            p_t = held("p%d" % t, [P, O], F32)
-            nc.vector.tensor_copy(p_t[:], acc[:])
-            nc.scalar.activation(out=pages[t][:].indirect(idx7[:]), in_=p_t[:], func=ACT.Copy, scale=so_c[:, t, :])
-            nc.sync.dma_start(out=out[cols, :], in_=pages[t][:])
+            nc.sync.dma_start(out=out[t * P : (t + 1) * P, :], in_=pages[t][:])

@@ -55,8 +55,8 @@ def tile_list_quarterlaws_kernel(
         sb_pool = ctx.enter_context(tc.tile_pool(name="held", bufs=1))
         psum = ctx.enter_context(tc.psum_pool(name="psum", bufs=1))
 
-        def held(name, shape, dtype):
-            return sb_pool.tile(shape, dtype, name=name, align_bytes=64)
+        def held(name, shape, dtype, tag=None):
+            return sb_pool.tile(shape, dtype, name=name, tag=tag or name, align_bytes=64)
 
         def load_list(name, src):
             lst = held(name, list(src.shape), U16)
@@ -88,11 +88,12 @@ def tile_list_quarterlaws_kernel(
         for page in pages:
             nc.vector.memset(page[:], 0.0)
 
-        sy, gp = nc.sync, nc.gpsimd
-        stage_scale_rows(sy, ww_stage[:, :, 0 : R // 4], w_scales)
-        stage_scale_rows(sy, ww_stage[:, :, R // 4 : 2 * R // 4], w0_scales)
+        sy, sc, gp = nc.sync, nc.sync, nc.gpsimd
+        stage_scale_rows(sc, ww_stage[:, :, 0 : R // 4], w_scales)
+        stage_scale_rows(sc, ww_stage[:, :, R // 4 : 2 * R // 4], w0_scales)
         idx = load_list("idx", offs)
-        load_scale_rows(sy, xt_s, xt_scales, (0, 1, 2, 3))
+        load_scale_rows(sy, xt_s, xt_scales, (0, 1, 2))
+        load_scale_rows(sc, xt_s, xt_scales, (3,))
         sy.dma_start(out=xt_w[:].bitcast(I32), in_=xt_words[0].rearrange("p c r -> p (c r)").bitcast(I32))
         idx2 = load_list("idx2", offs2)
         sy.dma_start(out=xo_w[:].bitcast(I32), in_=xo_words[0].bitcast(I32))
@@ -122,21 +123,39 @@ def tile_list_quarterlaws_kernel(
         xo_sg = held("xo_sg", [P, J], U8)
         xo_wg = held("xo_wg", [P, J], U16)
         nc.vector.tensor_copy(xt_sg[:], xt_s[:].indirect(idx[:]))
-        ww_sd = held("ww_sd", [P, 2, QUARTERS, P], U8)
-        nc.vector.tensor_copy(
-            out=ww_sd[:].rearrange("p m g q -> p m q g"),
-            in_=ww_s[:].rearrange("p (m q g) -> p m q g", m=2, g=QUARTERS),
-        )
+        ww_sd = {}
+
+        def deal_scales(quarters, tag):
+            picked = range(QUARTERS)[quarters]
+            dealt = held("ww_sd%d" % picked[0], [P, len(picked), 2, P], U8, tag)
+            nc.vector.tensor_copy(
+                out=dealt[:], in_=ww_s[:].rearrange("p (m q g) -> p g m q", m=2, g=QUARTERS)[:, quarters, :, :]
+            )
+            for i, g in enumerate(picked):
+                ww_sd[g] = dealt[:, i, :, :]
+
+        deal_scales(slice(2, 3), None)
         nc.vector.tensor_copy(xt_wg[:], xt_w[:].indirect(idx[:]))
         nc.vector.tensor_copy(xo_wg[:], xo_w[:].indirect(idx2[:]))
         nc.vector.tensor_copy(xo_sg[:], xo_s[:].indirect(idx2[:]))
+        deal_scales(slice(0, 4, 3), "xo_s")
 
-        w_wd = held("w_wd", [P, QUARTERS, P], U16)
-        nc.scalar.copy(out=w_wd[:].rearrange("p g q -> p q g"), in_=w_w[:].rearrange("p (q g) -> p q g", g=QUARTERS))
-        w0_wd = {}
-        for g in (2, 3, 0, 1):
-            w0_wd[g] = held("w0_wd%d" % g, [P, P], U32)
-            nc.scalar.copy(out=w0_wd[g][:], in_=w0_w[:, g:R:QUARTERS])
+        def deal_words(name, words, dtype, first, count):
+            dealt = held("%s%d" % (name, first), [P, count, P], dtype)
+            nc.scalar.copy(
+                out=dealt[:].rearrange("p g q -> p q g"),
+                in_=words[:].rearrange("p (q g) -> p q g", g=QUARTERS)[:, :, first : first + count],
+            )
+            return {first + i: dealt[:, i, :] for i in range(count)}
+
+        w_wd, w0_wd = {}, {}
+        for name, words, dtype, dealt, parts in (
+            ("w_wd", w_w, U16, w_wd, ((2, 2), (0, 2))),
+            ("w0_wd", w0_w, U32, w0_wd, ((2, 1), (3, 1), (0, 2))),
+        ):
+            for first, count in parts:
+                for g, part in deal_words(name, words, dtype, first, count).items():
+                    dealt[g] = part
 
         hid = held("hid", [P, O * QUARTERS], BF16)
         laws = (
@@ -145,21 +164,24 @@ def tile_list_quarterlaws_kernel(
             (0, idx3, ACT.Copy, dict(scale=sa_c[:])),
             (1, idx4, ACT.Copy, dict(scale=sb_c[:])),
         )
-        acc_of = {}
-        for g, lst, func, affine in laws:
-            acc_of[g] = psum.tile([P, J], F32, name="acc%d" % g)
-            nc.tensor.matmul_mx(
-                out=acc_of[g][:], lhsT=w_wd[:, g, :].bitcast(E2M1X4), lhsT_scale=ww_sd[:, 0, g, :],
-                rhs=xt_wg[:].bitcast(E4M3X4), rhs_scale=xt_sg[:], start=True, stop=False,
-            )
         a_of = {}
-        for g, lst, func, affine in laws:
-            nc.tensor.matmul_mx(
-                out=acc_of[g][:], lhsT=w0_wd[g][:].bitcast(E4M3X4), lhsT_scale=ww_sd[:, 1, g, :],
-                rhs=xo_wg[:].bitcast(E2M1X4), rhs_scale=xo_sg[:], start=False, stop=True,
+        for g in (2, 3, 0, 1):
+            acc = psum.tile([P, J], F32, name="acc%d" % g)
+            tokens = dict(
+                lhsT=w_wd[g].bitcast(E2M1X4), lhsT_scale=ww_sd[g][:, 0, :],
+                rhs=xt_wg[:].bitcast(E4M3X4), rhs_scale=xt_sg[:],
             )
+            notes = dict(
+                lhsT=w0_wd[g].bitcast(E4M3X4), lhsT_scale=ww_sd[g][:, 1, :],
+                rhs=xo_wg[:].bitcast(E2M1X4), rhs_scale=xo_sg[:],
+            )
+            opening, closing = (tokens, notes) if g == 2 else (notes, tokens)
+            nc.tensor.matmul_mx(out=acc[:], start=True, stop=False, **opening)
+            nc.tensor.matmul_mx(out=acc[:], start=False, stop=True, **closing)
             a_of[g] = held("a%d" % g, [P, J], F32)
-            nc.vector.tensor_copy(a_of[g][:], acc_of[g][:])
+            nc.vector.tensor_copy(a_of[g][:], acc[:])
+            if g == 2:
+                deal_scales(slice(1, 2), "ww_sd2")
 
         def fetch(law, first, count):
             g, lst, func, affine = law

from contextlib import ExitStack

import concourse.mybir as mybir

F32 = mybir.dt.float32
BF16 = mybir.dt.bfloat16
I32 = mybir.dt.int32
U32 = mybir.dt.uint32
U16 = mybir.dt.uint16
U8 = mybir.dt.uint8
E4M3X4 = mybir.dt.float8_e4m3fn_x4
E2M1X4 = mybir.dt.float4_e2m1fn_x4
ACT = mybir.ActivationFunctionType

P = 128
T, J, R, O, N, E = 1024, 256, 512, 128, 256, 256
QUARTERS = 4
QUADRANTS = 4
HALF = O // 2
FLOPS = 2 * 512 * R * J * 2 + 2 * R * N * O


def load_scale_rows(queue, plane, scales, quadrants):
    for quad in quadrants:
        queue.dma_start(
            out=plane[32 * quad : 32 * quad + 32, :].bitcast(I32),
            in_=scales[:, 4 * quad : 4 * quad + 4, :].bitcast(I32).to_broadcast([8, 4, scales.shape[2] // 4]),
        )


def load_live_scale_rows(queue, plane, scales, quadrants):
    for quad in quadrants:
        queue.dma_start(
            out=plane[32 * quad : 32 * quad + 4, :].bitcast(I32),
            in_=scales[0, 4 * quad : 4 * quad + 4, :].bitcast(I32),
        )


def stage_scale_rows(queue, stage, scales):
    queue.dma_start(out=stage, in_=scales[0].bitcast(I32).rearrange("(a r) c -> r a c", r=4))


def spread_scale_rows(nc, plane, stage):
    for quad in range(QUADRANTS):
        nc.vector.tensor_copy(plane[32 * quad : 32 * quad + 4, :].bitcast(I32), stage[:, quad, :])


def tile_list_quarterlaws_kernel(
    tc, xt_words, xt_scales, xo_words, xo_scales, w_words, w_scales, w0_words, w0_scales,
    sa, sb, sd, bd, se, be, wb_words, wb_scales, so,
    offs, offs2, offs3, offs4, offs5, offs6, offs7, out,
):
    nc = tc.nc
    with ExitStack() as ctx:
        sb_pool = ctx.enter_context(tc.tile_pool(name="held", bufs=1))
        psum = ctx.enter_context(tc.psum_pool(name="psum", bufs=1))

        def held(name, shape, dtype, tag=None):
            return sb_pool.tile(shape, dtype, name=name, tag=tag or name, align_bytes=64)

        def load_list(name, src):
            lst = held(name, list(src.shape), U16)
            nc.sync.dma_start(lst[:], src)
            return lst

        def load_column(queue, name, src):
            col = held(name, [P, 1], F32)
            queue.dma_start(out=col[:], in_=src)
            return col

        xt_w = held("xt_w", [P, T], U32)
        xo_w = held("xo_w", [P, T], U16)
        w_w = held("w_w", [P, R], U16)
        w0_w = held("w0_w", [P, R], U32)
        wb_w = held("wb_w", [P, N], U32)
        xt_s = held("xt_s", [P, T], U8)
        xo_s = held("xo_s", [P, T], U8)
        ww_s = held("ww_s", [P, 2 * R], U8)
        ww_stage = held("ww_stage", [4, QUADRANTS, 2 * R // 4], I32)
        wb_stage = held("wb_stage", [4, QUADRANTS, N // 4], I32)
        wb_s = held("wb_s", [P, N], U8)
        pages = [held("page%d" % t, [P, E], F32) for t in range(N // P)]

        nc.vector.memset(xo_s[0:64, :].bitcast(I32), 0)
        nc.vector.memset(xo_s[64:96, :].bitcast(I32), 0)
        for plane in (ww_s, wb_s):
            nc.vector.memset(plane[:].bitcast(I32), 0)
        for page in pages:
            nc.vector.memset(page[:], 0.0)

        sy, sc, gp = nc.sync, nc.sync, nc.gpsimd
        stage_scale_rows(sc, ww_stage[:, :, 0 : R // 4], w_scales)
        stage_scale_rows(sc, ww_stage[:, :, R // 4 : 2 * R // 4], w0_scales)
        idx = load_list("idx", offs)
        load_scale_rows(sy, xt_s, xt_scales, (0, 1, 2))
        load_scale_rows(sc, xt_s, xt_scales, (3,))
        sy.dma_start(out=xt_w[:].bitcast(I32), in_=xt_words[0].rearrange("p c r -> p (c r)").bitcast(I32))
        idx2 = load_list("idx2", offs2)
        sy.dma_start(out=xo_w[:].bitcast(I32), in_=xo_words[0].bitcast(I32))
        sy.dma_start(out=w_w[:].bitcast(I32), in_=w_words[0].bitcast(I32))
        load_live_scale_rows(sy, xo_s, xo_scales, (0, 1, 2))
        load_scale_rows(gp, xo_s, xo_scales, (3,))
        sy.dma_start(out=w0_w[:].bitcast(I32), in_=w0_words[0].rearrange("p c r -> p (c r)").bitcast(I32))
        idx5 = load_list("idx5", offs5)
        sd_c = load_column(sy, "sd_c", sd)
        bd_c = load_column(sy, "bd_c", bd)
        idx6 = load_list("idx6", offs6)
        se_c = load_column(sy, "se_c", se)
        be_c = load_column(sy, "be_c", be)
        idx3 = load_list("idx3", offs3)
        idx4 = load_list("idx4", offs4)
        stage_scale_rows(sy, wb_stage[:], wb_scales)
        sy.dma_start(out=wb_w[:].bitcast(I32), in_=wb_words[0].rearrange("p c r -> p (c r)").bitcast(I32))
        idx7 = load_list("idx7", offs7)
        sa_c = load_column(gp, "sa_c", sa)
        sb_c = load_column(gp, "sb_c", sb)
        so_c = held("so_c", [P, N // P, 1], F32)
        gp.dma_start(out=so_c[:], in_=so.rearrange("(t p) o -> p t o", p=P))

        spread_scale_rows(nc, ww_s, ww_stage)
        xt_sg = held("xt_sg", [P, J], U8)
        xt_wg = held("xt_wg", [P, J], U32)
        xo_sg = held("xo_sg", [P, J], U8)
        xo_wg = held("xo_wg", [P, J], U16)
        nc.vector.tensor_copy(xt_sg[:], xt_s[:].indirect(idx[:]))
        ww_sd = {}

        def deal_scales(quarters, tag):
            picked = range(QUARTERS)[quarters]
            dealt = held("ww_sd%d" % picked[0], [P, len(picked), 2, P], U8, tag)
            nc.vector.tensor_copy(
                out=dealt[:], in_=ww_s[:].rearrange("p (m q g) -> p g m q", m=2, g=QUARTERS)[:, quarters, :, :]
            )
            for i, g in enumerate(picked):
                ww_sd[g] = dealt[:, i, :, :]

        deal_scales(slice(2, 3), None)
        nc.vector.tensor_copy(xt_wg[:], xt_w[:].indirect(idx[:]))
        nc.vector.tensor_copy(xo_wg[:], xo_w[:].indirect(idx2[:]))
        nc.vector.tensor_copy(xo_sg[:], xo_s[:].indirect(idx2[:]))
        deal_scales(slice(0, 4, 3), "xo_s")

        def deal_words(name, words, dtype, first, count):
            dealt = held("%s%d" % (name, first), [P, count, P], dtype)
            nc.scalar.copy(
                out=dealt[:].rearrange("p g q -> p q g"),
                in_=words[:].rearrange("p (q g) -> p q g", g=QUARTERS)[:, :, first : first + count],
            )
            return {first + i: dealt[:, i, :] for i in range(count)}

        w_wd, w0_wd = {}, {}
        for name, words, dtype, dealt, parts in (
            ("w_wd", w_w, U16, w_wd, ((2, 2), (0, 2))),
            ("w0_wd", w0_w, U32, w0_wd, ((2, 1), (3, 1), (0, 2))),
        ):
            for first, count in parts:
                for g, part in deal_words(name, words, dtype, first, count).items():
                    dealt[g] = part

        hid = held("hid", [P, O * QUARTERS], BF16)
        laws = (
            (2, idx5, ACT.Exp, dict(scale=sd_c[:], bias=bd_c[:])),
            (3, idx6, ACT.Sigmoid, dict(scale=se_c[:], bias=be_c[:])),
            (0, idx3, ACT.Copy, dict(scale=sa_c[:])),
            (1, idx4, ACT.Copy, dict(scale=sb_c[:])),
        )
        a_of = {}
        for g in (2, 3, 0, 1):
            acc = psum.tile([P, J], F32, name="acc%d" % g)
            tokens = dict(
                lhsT=w_wd[g].bitcast(E2M1X4), lhsT_scale=ww_sd[g][:, 0, :],
                rhs=xt_wg[:].bitcast(E4M3X4), rhs_scale=xt_sg[:],
            )
            notes = dict(
                lhsT=w0_wd[g].bitcast(E4M3X4), lhsT_scale=ww_sd[g][:, 1, :],
                rhs=xo_wg[:].bitcast(E2M1X4), rhs_scale=xo_sg[:],
            )
            opening, closing = (tokens, notes) if g == 2 else (notes, tokens)
            nc.tensor.matmul_mx(out=acc[:], start=True, stop=False, **opening)
            nc.tensor.matmul_mx(out=acc[:], start=False, stop=True, **closing)
            a_of[g] = held("a%d" % g, [P, J], F32)
            nc.vector.tensor_copy(a_of[g][:], acc[:])
            if g == 2:
                deal_scales(slice(1, 2), "ww_sd2")

        def fetch(law, first, count):
            g, lst, func, affine = law
            nc.scalar.activation(
                out=hid[:, QUARTERS * first + g : QUARTERS * (first + count) : QUARTERS],
                in_=a_of[g][:].indirect(lst[:, first // 16 : (first + count) // 16]), func=func, **affine,
            )

        fetch(laws[0], 0, O)
        for half in range(2):
            for law in laws[1:]:
                fetch(law, half * HALF, HALF)

        spread_scale_rows(nc, wb_s, wb_stage)
        for half in range(2):
            hid_w = held("hid_w%d" % half, [P, HALF], U32)
            hid_s = held("hid_s%d" % half, [P, HALF], U8)
            nc.vector.quantize_mx(
                out=hid_w[:].bitcast(E4M3X4), scales=hid_s[:],
                in_=hid[:, QUARTERS * HALF * half : QUARTERS * HALF * (half + 1)],
            )
            for t in range(N // P):
                cols = slice(t * P, (t + 1) * P)
                acc = psum.tile([P, HALF], F32, name="pacc%d%d" % (half, t))
                nc.tensor.matmul_mx(
                    out=acc[:], lhsT=wb_w[:, cols].bitcast(E4M3X4), lhsT_scale=wb_s[:, cols],
                    rhs=hid_w[:].bitcast(E4M3X4), rhs_scale=hid_s[:], start=True, stop=True,
                )
                p_part = held("p%d%d" % (half, t), [P, HALF], F32)
                nc.vector.tensor_copy(p_part[:], acc[:])
                nc.scalar.activation(
                    out=pages[t][:].indirect(idx7[:, half * HALF // 16 : (half + 1) * HALF // 16]),
                    in_=p_part[:], func=ACT.Copy, scale=so_c[:, t, :],
                )
        for t in range(N // P):
            nc.sync.dma_start(out=out[t * P : (t + 1) * P, :], in_=pages[t][:])
